import numpy as np, ml_dtypes
CORES = [0,11,22,25,36,47,50,61,64,75,86,89]
N = 12
MB, TK = 16, 64
def setup_inputs(rng):
    return {"x": rng.standard_normal((N, MB, 128, TK), dtype=np.float32).astype(ml_dtypes.bfloat16), "w": (rng.standard_normal((N, 128, 128), dtype=np.float32) / 8).astype(ml_dtypes.bfloat16)}
def reference(x, w):
    def run(a, W, order):
        for s in order:
            a = np.maximum(np.einsum("kf,bkn->bfn", W[s].astype(np.float64), a), 0.0)
        return a
    dt = ml_dtypes.bfloat16 if x.dtype != np.float64 else np.float64
    y = np.full(x.shape, np.nan, dt)
    y[N - 1] = run(x[0].astype(np.float64), w, range(N)).astype(dt)
    return {"y": y}

from concourse.bass import DstId, RemoteDMATransfer
from concourse.mybir import AluOpType
import comms_topo

CORES = [0, 11, 22, 25, 36, 47, 50, 61, 64, 75, 86, 89]
N, MB, TK = 12, 16, 64
WORKERS = [19, 39, 51, 87, 15, 41, 59, 79]
XRELAYS = [3, 7]
PER = 2
OUT_TILE = True
P = len(WORKERS)
MBW = MB // P
KP = 128 // MBW
TW = MBW * TK
LAST = CORES[-1]


def _interleave(cand, k):
    a = [c for c in cand if c // 4 == k // 4]
    b = [c for c in cand if c // 4 != k // 4]
    if k in a:
        a.remove(k)
        a.insert(0, k)
    out = []
    for i in range(max(len(a), len(b))):
        out += a[i:i + 1] + b[i:i + 1]
    return out


def _links(a, b):
    ca, cb, d, out = a // 8, b // 8, comms_topo.die(a), []
    if ca == cb:
        return out
    if (ca & 1) != (cb & 1):
        out.append(("mate", ca, d))
        ca ^= 1
    if ca != cb:
        out += [("out", ca, d), ("in", cb, d)]
    return out


def build_plan():
    load = {}

    def add(ld, a, b, n):
        for l in _links(a, b):
            ld[l] = ld.get(l, 0) + n

    xdirect, xrelay = [], {}
    i = 0
    for j, w in enumerate(WORKERS):
        if comms_topo.may_write(CORES[0], w):
            xdirect.append((j, w))
            add(load, CORES[0], w, 1)
        else:
            rc = XRELAYS[i % len(XRELAYS)]
            xrelay.setdefault(rc, []).append((j, w))
            add(load, rc, w, 1)
            i += 1
    busy = set(WORKERS) | set(XRELAYS) | set(CORES[0:1])
    send, helpers = {}, {}
    for s, r in enumerate(CORES):
        ch, k = divmod(r, 8)
        same = [w for w in WORKERS if ((w // 8) & 1) == (ch & 1)]
        cross = [w for w in WORKERS if ((w // 8) & 1) != (ch & 1)]
        used = []
        helpers[s] = []
        for grp, cand in ((cross, (2, 6, 3, 7)), (same, (0, 4, 1, 5, 2, 6, 3, 7))):
            if not grp:
                continue
            cand = [c for c in cand if ch * 8 + c not in busy and c not in used]
            if grp is same and cross and k in (0, 1, 4, 5):
                cand = [c for c in cand if c in (0, 1, 4, 5)]
            order = _interleave(cand, k)
            n = -(-len(grp) // PER)
            best = None
            for rot in range(len(grp)):
                g2 = grp[rot:] + grp[:rot]
                l2 = dict(load)
                for t in range(n):
                    for w in g2[t * PER:(t + 1) * PER]:
                        add(l2, ch * 8 + order[t], w, MBW if s == 0 else 1)
                key = (max(l2.values()), sum(v * v for v in l2.values()))
                if best is None or key < best[0]:
                    best = (key, g2, l2)
            g2, load = best[1], best[2]
            for t in range(n):
                c = order[t]
                used.append(c)
                send[ch * 8 + c] = (s, g2[t * PER:(t + 1) * PER])
                if ch * 8 + c != r:
                    helpers[s].append(ch * 8 + c)
    return send, helpers, xdirect, xrelay


SEND, HELPERS, XDIRECT, XRELAY = build_plan()
XSLOTS = max([1] + [len(v) for v in XRELAY.values()])

SCRATCH = {
    "wd": ("dram", [128, 128], "bfloat16"),
    "wd0": ("dram", [128, MBW * 128], "bfloat16"),
    "xd": ("dram", [P, 128, TW], "bfloat16"),
    "xin": ("dram", [XSLOTS, 128, TW], "bfloat16"),
    "xs": ("sbuf", [128, TW], "bfloat16"),
    "w0s": ("sbuf", [128, MBW * 128], "bfloat16"),
    "ws": ("sbuf", [128, (N - 1) * 128], "bfloat16"),
    "act": ("sbuf", [128, TW], "bfloat16"),
    "outb": ("sbuf", [128, TW], "bfloat16"),
    "zeros": ("sbuf", [128, TW], "bfloat16"),
    "pso": ("psum", [128, 512], "float32"),
    "yd": ("dram", [P, 128, TW] if OUT_TILE else [MB, 128, TK], "bfloat16"),
}
for _i in range(MBW):
    SCRATCH["ps%d" % _i] = ("psum", [128, 512], "float32")

SEMAPHORES = (["wl", "xl", "wa", "xa", "xsa", "z", "ls", "ya", "st", "to", "vo"]
              + ["w%d" % s for s in range(N)] + ["t%d" % i for i in range(MBW)] + ["v%d" % i for i in range(MBW)])


def _pow2(n):
    p = 1
    while p * 2 <= n:
        p *= 2
    return p


def _masks(n, base, width):
    e = _pow2(width // n)
    return e, [((1 << e) - 1) << (base + i * e) for i in range(n)]


def x_counts():
    items = [(j, w, 0) for j, w in XDIRECT]
    for rc, lst in XRELAY.items():
        items += [(j, rc, sl) for sl, (j, w) in enumerate(lst)]
    on = [it for it in items if it[1] // 8 == CORES[0] // 8]
    off = [it for it in items if it[1] // 8 != CORES[0] // 8]
    tr, cnt = [], {}
    for lst, base in ((off, 0), (on, 8 if off else 0)):
        if not lst:
            continue
        e, ms = _masks(len(lst), base, 8 if (off or base) else 16)
        for it, m in zip(lst, ms):
            tr.append(it + (m,))
            cnt[it[1]] = cnt.get(it[1], 0) + e
    return tr, cnt


def y_mask(w):
    return 0xFFFF if w // 8 == LAST // 8 else 0x00FF


def rank_program(g, core, T, topo):
    S = T.sem
    rank = T.rank_of(core)
    nls = [0]

    def did(c):
        rid, pid, _se = topo.addr(c)
        return DstId(rid=rid, pnc=pid)

    def bits(m):
        return bin(m).count("1")

    def fused(trs):
        g.remote_dma_fused(trs, local_sem=S.ls)

    def one(src, dst, cores, mask, sem):
        nls[0] += bits(mask)
        return RemoteDMATransfer(dst_ids=[did(c) for c in cores], dma_engine_mask=mask, remote_sem=sem,
                                 srcs=[src], dsts=[dst for _c in cores], alu_op=0)

    xtr, xcnt = x_counts()

    if rank is not None:
        if rank == 0:
            for i in range(MBW):
                g.sync.dma_start(T.wd0[i * KP:(i + 1) * KP, :], T.w[:]).then_inc(S.wl, 16)
            g.scalar.dma_start(T.xd[:], T.x[:]).then_inc(S.xl, 16)
        else:
            g.sync.dma_start(T.wd[:], T.w[:]).then_inc(S.wl, 16)

    if core in WORKERS:
        j = WORKERS.index(core)
        te, ve = g.tensor, g.vector
        ps = [T["ps%d" % i] for i in range(MBW)]
        ts = [S["t%d" % i] for i in range(MBW)]
        vs = [S["v%d" % i] for i in range(MBW)]
        if core in xcnt:
            g.sync.wait_ge(S.xa, xcnt[core])
            g.sync.dma_start(T.xs[:], T.xin[0]).then_inc(S.xsa, 16)
            nx = 16
        else:
            nx = _masks(XSLOTS, 0, 8)[0]
        ve.memset(T.zeros[:], 0.0).then_inc(S.z, 1)
        ve.wait_ge(S.z, 1)
        nlay = N - 1 if OUT_TILE else N
        te.wait_ge(S.xsa, nx)
        te.wait_ge(S.w0, 8)
        for i in range(MBW):
            for q in range(MBW):
                mm = te.matmul(ps[i][:, 0:TK], T.w0s[i * KP:(i + 1) * KP, q * 128:(q + 1) * 128],
                               T.xs[i * KP:(i + 1) * KP, q * TK:(q + 1) * TK], q == 0, q == MBW - 1)
            mm.then_inc(ts[i], 1)
        for s in range(1, nlay):
            te.wait_ge(S["w%d" % s], 8)
            for i in range(MBW):
                te.wait_ge(vs[i], s)
                te.matmul(ps[i][:, 0:TK], T.ws[:, (s - 1) * 128:s * 128], T.act[:, i * TK:(i + 1) * TK],
                          True, True).then_inc(ts[i], 1)
        for s in range(nlay):
            for i in range(MBW):
                ve.wait_ge(ts[i], s + 1)
                o = T.outb if s == N - 1 else T.act
                ve.tensor_tensor(o[:, i * TK:(i + 1) * TK], ps[i][:, 0:TK], T.zeros[:, 0:TK],
                                 AluOpType.max).then_inc(vs[i], 1)
        if OUT_TILE:
            s = N - 1
            te.wait_ge(S["w%d" % s], 8)
            for i in range(MBW):
                te.wait_ge(vs[i], s)
                for q in range(MBW):
                    te.matmul(T.pso[i * KP:(i + 1) * KP, q * TK:(q + 1) * TK],
                              T.ws[:, (s - 1) * 128 + q:s * 128:MBW], T.act[:, i * TK:(i + 1) * TK],
                              True, True).then_inc(S.to, 1)
            ve.wait_ge(S.to, MBW * MBW)
            ve.tensor_tensor(T.outb[:], T.pso[:, 0:TW], T.zeros[:], AluOpType.max).then_inc(S.vo, 1)

    if rank is not None:
        g.wait_ge(S.wl, 16 * MBW if rank == 0 else 16)
        buf = T.wd0 if rank == 0 else T.wd
        if HELPERS[rank]:
            fused([one(buf[:], buf[:], HELPERS[rank], 0xFFFF, S.wa)])
    if core in SEND:
        s, ws_ = SEND[core]
        if rank is None:
            g.wait_ge(S.wa, 16)
        src = T.wd0[:] if s == 0 else T.wd[:]
        dst = T.w0s[:] if s == 0 else T.ws[:, (s - 1) * 128:s * 128]
        fused([one(src, dst, ws_, 0x00FF, S["w%d" % s])])
    if rank == 0:
        g.wait_ge(S.xl, 16)
        fused([one(T.xd[j], T.xin[sl], [c], m, S.xa) for (j, c, sl, m) in xtr])
    if core in XRELAY:
        lst = XRELAY[core]
        g.wait_ge(S.xa, xcnt[core])
        _e, ms = _masks(XSLOTS, 0, 8)
        fused([one(T.xin[sl], T.xs[:], [w], ms[sl], S.xsa) for sl, (j, w) in enumerate(lst)])
    if core in WORKERS:
        j = WORKERS.index(core)
        if OUT_TILE:
            g.wait_ge(S.vo, 1)
            fused([one(T.outb[:], T.yd[j], [LAST], y_mask(core), S.ya)])
        else:
            for i in range(MBW):
                g.wait_ge(S["v%d" % i], N)
            _e, ms = _masks(MBW, 0, bits(y_mask(core)))
            fused([one(T.outb[:, i * TK:(i + 1) * TK], T.yd[j * MBW + i], [LAST], ms[i], S.ya)
                   for i in range(MBW)])
    if core == LAST:
        g.sync.wait_ge(S.ya, sum(bits(y_mask(w)) for w in WORKERS))
        g.sync.dma_start(T.y[:], T.yd[:]).then_inc(S.st, 16)
        g.sync.wait_ge(S.st, 16)
    if nls[0]:
        g.wait_ge(S.ls, nls[0])
